import numpy as np
import ml_dtypes


def mxq(x, axis, fmt="e4m3"):
    dtype, down = {"e4m3": (ml_dtypes.float8_e4m3fn, 7), "e5m2": (ml_dtypes.float8_e5m2, 14)}[fmt]
    v = np.moveaxis(np.asarray(x, np.float32).astype(ml_dtypes.bfloat16).astype(np.float64), axis, -1)
    blocks = v.reshape(v.shape[:-1] + (-1, 32))
    amax = np.abs(blocks).max(-1, keepdims=True)
    byte = np.maximum(np.where(amax > 0, np.frexp(amax)[1] - 1 + 127, 0) - down, 1)
    scale = np.exp2(byte - 127.0)
    codes = (blocks / scale).astype(np.float32).astype(dtype).astype(np.float64)
    return np.moveaxis((codes * scale).reshape(v.shape), -1, axis)


WIDE = False


def mx_kscale(k):
    if not WIDE:
        return np.ones(k)
    levels = np.array([24, -24, 12, -12, 0])
    if k % 512:
        return np.exp2(np.random.permutation(np.resize(levels, k // 32))).repeat(32)
    a = np.empty((k // 512, 16))
    for p in range(k // 512):
        a[p, :8] = np.random.permutation(np.resize(levels, 8))
        for g in range(8):
            far = levels[np.abs(levels - a[p, g]) >= 10]
            a[p, g + 8] = far[np.random.randint(len(far))]
    return np.exp2(a.ravel()).repeat(32)


def f64(x):
    return np.asarray(x).astype(np.float64)


def striped(idx):
    return np.tile(idx.reshape(-1, 16).T, (8, 1)).astype(np.uint16)


def unstriped(offs):
    return offs[:16].T.reshape(-1).astype(np.int64)


E2M1 = np.array([0.0, 0.5, 1.0, 1.5, 2.0, 3.0, 4.0, 6.0, -0.0, -0.5, -1.0, -1.5, -2.0, -3.0, -4.0, -6.0])


def pack_weight(w, fmt):
    k, n = w.shape
    w = f64(np.asarray(w, np.float32).astype(ml_dtypes.bfloat16)).reshape(k // 32, 32, n)
    amax = np.abs(w).max(1)
    if fmt == "e4m3":
        byte = np.frexp(amax)[1] - 1 + 127 - 7
    else:
        mant, ex = np.frexp(amax / 6.0)
        byte = np.where(mant > 0.5, ex, ex - 1) + 127
    byte = np.clip(np.where(amax > 0, byte, 1), 1, 254)
    scaled = (w * np.exp2(127.0 - byte)[:, None, :]).reshape(k, n).astype(np.float32)
    by_word = np.ascontiguousarray(scaled.reshape(k // 512, 128, 4, n).transpose(0, 1, 3, 2))
    if fmt == "e4m3":
        words = by_word.astype(ml_dtypes.float8_e4m3fn).view(np.uint8)
    else:
        c = by_word.astype(ml_dtypes.float4_e2m1fn).view(np.uint8) & 0xF
        words = (c[..., 0::2] | (c[..., 1::2] << 4)).reshape(k // 512, 128, 2 * n)
    return np.ascontiguousarray(words), np.ascontiguousarray(byte.astype(np.uint8).reshape(k // 512, 16, n))


def unpack_weight(words, scales, fmt):
    g, _, n = scales.shape
    words = np.ascontiguousarray(words).reshape(g, 128, n, -1)
    if fmt == "e4m3":
        vals = words.view(ml_dtypes.float8_e4m3fn).astype(np.float64)
    else:
        nib = np.empty((g, 128, n, 4), np.uint8)
        nib[..., 0::2] = words & 0xF
        nib[..., 1::2] = words >> 4
        vals = E2M1[nib]
    vals = vals * np.repeat(np.exp2(scales.astype(np.float64) - 127.0), 8, axis=1)[..., None]
    return vals.transpose(0, 1, 3, 2).reshape(g * 512, n)


def pack_table4(v):
    words, scales = pack_weight(v, "e2m1")
    g, t = words.shape[0] // 2, v.shape[1]
    return np.ascontiguousarray(words.reshape(g, 2, 128, t, 2).transpose(0, 2, 3, 1, 4).reshape(g, 128, t, 4)), scales


def unpack_table4(words, scales):
    g, _, t, _ = words.shape
    return unpack_weight(words.reshape(g, 128, t, 2, 2).transpose(0, 3, 1, 2, 4).reshape(2 * g, 128, 2 * t), scales, "e2m1")


def planes(y):
    n, m = y.shape
    v = y.astype(np.float32).astype(ml_dtypes.bfloat16).astype(np.float64).reshape(n // 32, 32, m)
    top = np.abs(v).max(1)
    byte = np.clip(np.where(top > 0, np.frexp(top)[1] - 1 + 127 - 7, 1), 1, 254)
    codes = (v * np.exp2(127.0 - byte)[:, None, :]).reshape(n, m).astype(np.float32).astype(ml_dtypes.float8_e4m3fn).view(np.uint8)
    words = codes.reshape(n // 512, 128, 4, m).transpose(0, 1, 3, 2)
    return np.ascontiguousarray(words), np.ascontiguousarray(byte.astype(np.uint8).reshape(n // 512, 16, m))


K, M, N, T, J = 512, 1024, 1024, 2048, 1024


def setup_inputs():
    n = np.random.standard_normal
    s = mx_kscale(K)[:, None]
    s2 = mx_kscale(M)[:, None]
    h = np.tanh(n((N, T)))
    p_tab = pack_table4(h * s2)
    p_wn = pack_weight(n((K, N)) / np.sqrt(K) / s, "e4m3")
    p_un = pack_weight(n((M, N)) / np.sqrt(M) / s2, "e4m3")
    return {
        "x": (n((K, J)) * s).astype(np.float32),
        "tab_words": p_tab[0],
        "tab_scales": p_tab[1],
        "wn_words": p_wn[0],
        "wn_scales": p_wn[1],
        "un_words": p_un[0],
        "un_scales": p_un[1],
        "bn": (0.3 * n(N)).astype(np.float32),
        "hT": (h).astype(np.float32),
        "wgo": np.tile(np.random.uniform(0.5, 2.0, J), (128, 1)).astype(np.float32),
        "offs": striped(np.random.permutation(T)[:J]),
    }


def reference(x, tab_words, tab_scales, wn_words, wn_scales, un_words, un_scales, bn, hT, wgo, offs):
    idx = unstriped(offs)
    x_ = mxq(f64(x), 0, "e4m3")
    tab_ = unpack_table4(tab_words, tab_scales)[:, idx]
    wn_ = unpack_weight(wn_words, wn_scales, "e4m3")
    un_ = unpack_weight(un_words, un_scales, "e4m3")
    sn = wn_.T @ x_ + un_.T @ tab_
    out = np.zeros((N, T))
    out[:, idx] = f64(wgo)[0] * (np.tanh(sn + f64(bn)[:, None]) + f64(hT)[:, idx])
    return (out,) + planes(out)

@@ -1,0 +1,250 @@
+from contextlib import ExitStack
+
+import concourse.mybir as mybir
+
+K, M, N, T, J = 512, 1024, 1024, 2048, 1024
+FLOPS = 2 * (K + M) * N * J
+
+F32 = mybir.dt.float32
+BF16 = mybir.dt.bfloat16
+I32 = mybir.dt.int32
+U32 = mybir.dt.uint32
+U16 = mybir.dt.uint16
+U8 = mybir.dt.uint8
+FP8X4 = mybir.dt.float8_e4m3fn_x4
+FP4X4 = mybir.dt.float4_e2m1fn_x4
+ADD = mybir.AluOpType.add
+MULT = mybir.AluOpType.mult
+TANH = mybir.ActivationFunctionType.Tanh
+
+P = 128
+PACK = 4
+K_PASS = P * PACK
+HALF = 512
+QUARTER = 256
+CHUNK = 512
+GROUPS = N // K_PASS
+BYTE_ORDER = (2, 0, 1, 3)
+PAGES = 3
+VECTOR_CHUNKS = 2
+
+
+def tile_list_tgn_rnnP_kernel(
+    tc, x, tab_words, tab_scales, wn_words, wn_scales, un_words, un_scales, bn, hT, wgo, offs, out_0, out_1, out_2
+):
+    nc = tc.nc
+    slices = [(g, t) for g in range(GROUPS) for t in BYTE_ORDER]
+    halves = [slice(h * HALF, (h + 1) * HALF) for h in range(J // HALF)]
+    chunks = [slice(c * CHUNK, (c + 1) * CHUNK) for c in range(T // CHUNK)]
+
+    with ExitStack() as ctx:
+        keep = ctx.enter_context(tc.tile_pool(name="keep", bufs=1))
+        ring = ctx.enter_context(tc.tile_pool(name="ring", bufs=4))
+        psum = ctx.enter_context(tc.psum_pool(name="psum", bufs=8))
+
+        offsets = keep.tile([P, J // 16], U16, name="offsets")
+        nc.sync.dma_start(offsets[:], offs)
+        half_offsets = [offsets[:, h * (HALF // 16) : (h + 1) * (HALF // 16)] for h in range(J // HALF)]
+
+        tab_sc = keep.tile([P, T], U8, name="tab_sc", align_bytes=64)
+        w_sc_raw = keep.tile([P, 2, N], U8, name="w_sc_raw", align_bytes=64)
+        v_sc1 = keep.tile([P, J], U8, name="v_sc1", align_bytes=64)
+        nc.vector.memset(tab_sc[:].bitcast(I32), 0)
+        nc.gpsimd.memset(w_sc_raw[:].bitcast(I32), 0)
+        nc.vector.memset(v_sc1[:].bitcast(I32), 0)
+        pages = [keep.tile([P, T], F32, name="page%d" % b) for b in range(PAGES - 1)]
+        for page in pages:
+            nc.vector.memset(page[:], 0.0)
+
+        for q in range(4):
+            nc.sync.dma_start(
+                tab_sc[32 * q : 32 * q + 8, :].bitcast(I32), tab_scales[:, 4 * q : 4 * q + 4, :].bitcast(I32)
+            )
+        tab_w = keep.tile([P, T], I32, name="tab_w", align_bytes=64)
+        nc.sync.dma_start(tab_w[:], tab_words[0].rearrange("p t i -> p (t i)").bitcast(I32))
+        for q in range(4):
+            nc.sync.dma_start(
+                w_sc_raw[32 * q : 32 * q + 4, :, :].bitcast(I32),
+                un_scales[:, 4 * q : 4 * q + 4, :].rearrange("a r n -> r a n").bitcast(I32),
+            )
+            nc.sync.dma_start(
+                w_sc_raw[32 * q + 4 : 32 * q + 8, 0, :].bitcast(I32), wn_scales[0, 4 * q : 4 * q + 4, :].bitcast(I32)
+            )
+
+        x_rows = x.rearrange("(p i) j -> p i j", i=PACK)
+        x_raw = [keep.tile([P, PACK, QUARTER], F32, name="x_raw%d" % c) for c in range(J // QUARTER)]
+
+        def load_x(c):
+            nc.sync.dma_start(x_raw[c][:], x_rows[:, :, c * QUARTER : (c + 1) * QUARTER])
+
+        un_i32 = un_words.rearrange("a p n i -> p a (n i)").bitcast(I32)
+        wn_i32 = wn_words[0].rearrange("p n i -> p (n i)").bitcast(I32)
+        w_raw = [keep.tile([P, 3, K_PASS], U32, name="w_raw%d" % g) for g in range(GROUPS)]
+
+        def load_w(g):
+            cols = slice(g * K_PASS, (g + 1) * K_PASS)
+            nc.sync.dma_start(w_raw[g][:, 0:2, :].bitcast(I32), un_i32[:, :, cols])
+            nc.sync.dma_start(w_raw[g][:, 2, :].bitcast(I32), wn_i32[:, cols])
+
+        h_rows = hT.rearrange("(g p t) c -> g t p c", p=P, t=PACK)
+        out_rows = out_0.rearrange("(g p t) c -> g t p c", p=P, t=PACK)
+        state = {}
+
+        def load_state(i):
+            g, t = slices[i]
+            if i == 0:
+                state[i] = keep.tile([P, T], F32, name="state_first", tag="state_then_page")
+            else:
+                state[i] = ring.tile([P, T], F32, name="state")
+            nc.sync.dma_start(state[i][:], h_rows[g, t])
+
+        weight = keep.tile([P, J], F32, name="weight")
+        bias = keep.tile([P, GROUPS, PACK], F32, name="bias")
+
+        load_x(0)
+        load_x(1)
+        load_w(0)
+        nc.sync.dma_start(bias[:], bn.rearrange("(g p t) -> p g t", p=P, t=PACK))
+        load_state(0)
+        nc.sync.dma_start(weight[:, halves[0]], wgo[:, halves[0]])
+
+        v_sc0 = keep.tile([P, J], U8, name="v_sc0", align_bytes=64)
+        nc.vector.tensor_copy(v_sc0[:], tab_sc[:].indirect(offsets[:]))
+        for q in range(4):
+            nc.sync.dma_start(v_sc1[32 * q : 32 * q + 4, :].bitcast(I32), v_sc0[32 * q + 4 : 32 * q + 8, :].bitcast(I32))
+        v_sc = [v_sc0, v_sc1]
+
+        load_x(2)
+        load_x(3)
+        nc.sync.dma_start(weight[:, halves[1]], wgo[:, halves[1]])
+        load_state(1)
+        load_w(1)
+
+        w_sc = keep.tile([P, 2, N], U8, name="w_sc", align_bytes=64)
+        v_words = [keep.tile([P, 2, HALF], U16, name="v_words%d" % h, align_bytes=64) for h in range(2)]
+        x_codes = [keep.tile([P, HALF], U32, name="x_codes%d" % h, align_bytes=64) for h in range(2)]
+        x_sc = [keep.tile([P, HALF], U8, name="x_sc%d" % h, align_bytes=64) for h in range(2)]
+
+        def gather_table(h):
+            picked = keep.tile([P, HALF], U32, name="picked%d" % h, align_bytes=64)
+            nc.vector.tensor_copy(picked[:], tab_w[:].bitcast(U32).indirect(half_offsets[h]))
+            nc.vector.tensor_copy(v_words[h][:], picked[:].bitcast(U16).rearrange("p (j d) -> p d j", d=2))
+
+        def quantize_x(h):
+            grouped = keep.tile([P, HALF, PACK], BF16, name="x_grouped%d" % h, align_bytes=64)
+            for c in range(2):
+                nc.scalar.copy(
+                    grouped[:, c * QUARTER : (c + 1) * QUARTER, :].rearrange("p (c u) i -> p c i u", u=4),
+                    x_raw[2 * h + c][:].rearrange("p i (c u) -> p c i u", u=4),
+                )
+            nc.vector.quantize_mx(
+                out=x_codes[h][:].bitcast(FP8X4), scales=x_sc[h][:], in_=grouped[:].rearrange("p j i -> p (j i)")
+            )
+
+        w_dealt = {}
+        act = {}
+
+        def deal(i):
+            g, t = slices[i]
+            w_dealt[i] = keep.tile([P, 3, P], U32, name="w_dealt%d" % i, align_bytes=64)
+            nc.scalar.copy(w_dealt[i][:], w_raw[g][:].rearrange("p a (m t) -> p a t m", t=PACK)[:, :, t, :])
+            act[i] = ring.tile([P, J], F32, name="act")
+
+        def product(i, h):
+            g, t = slices[i]
+            cols = slice(g * K_PASS + t * P, g * K_PASS + (t + 1) * P)
+            acc = psum.tile([P, HALF], F32, name="acc")
+            for a in range(2):
+                nc.tensor.matmul_mx(
+                    out=acc[:],
+                    lhsT=w_dealt[i][:, a, :].bitcast(FP8X4),
+                    lhsT_scale=w_sc[:, a, cols],
+                    rhs=v_words[h][:, a, :].bitcast(FP4X4),
+                    rhs_scale=v_sc[a][:, halves[h]],
+                    start=(a == 0),
+                    stop=False,
+                )
+            nc.tensor.matmul_mx(
+                out=acc[:],
+                lhsT=w_dealt[i][:, 2, :].bitcast(FP8X4),
+                lhsT_scale=w_sc[4:P, 0, cols],
+                rhs=x_codes[h][:].bitcast(FP8X4),
+                rhs_scale=x_sc[h][:],
+                start=False,
+                stop=True,
+            )
+            nc.scalar.activation(act[i][:, halves[h]], acc[:], TANH, bias=bias[:, g, t : t + 1])
+
+        gather_table(0)
+        nc.vector.tensor_copy(
+            w_sc[:].rearrange("p a (g t m) -> p (a g) t m", t=PACK, m=P),
+            w_sc_raw[:].rearrange("p a (g m t) -> p (a g) t m", t=PACK, m=P),
+        )
+        quantize_x(0)
+        deal(0)
+        product(0, 0)
+        gather_table(1)
+        quantize_x(1)
+        product(0, 1)
+        deal(1)
+        product(1, 0)
+        product(1, 1)
+
+        grouped_out = {}
+        summed = {}
+
+        def place(i):
+            page = pages[i % PAGES]
+            if i == PACK:
+                summed[i] = keep.tile([P, J], F32, name="summed_mid", tag="summed_then_scales", align_bytes=64)
+            else:
+                summed[i] = ring.tile([P, J], F32, name="summed", bufs=2)
+            parts = list(zip(halves, half_offsets)) if i == 0 else [(slice(0, J), offsets[:])]
+            for cols, offs_part in parts:
+                nc.vector.tensor_tensor(summed[i][:, cols], state[i][:].indirect(offs_part), act[i][:, cols], ADD)
+                nc.vector.tensor_tensor(page[:].indirect(offs_part), summed[i][:, cols], weight[:, cols], MULT)
+
+        def hand_out(i):
+            g, t = slices[i]
+            page = pages[i % PAGES]
+            nc.scalar.dma_start(out_rows[g, t], page[:])
+            for c, cols in enumerate(chunks):
+                if (g, c) not in grouped_out:
+                    grouped_out[g, c] = keep.tile([P, CHUNK, PACK], BF16, name="grouped%d_%d" % (g, c), align_bytes=64)
+                if i == len(slices) - 1 and c < VECTOR_CHUNKS:
+                    nc.vector.tensor_copy(grouped_out[g, c][:, :, t], page[:, cols])
+                else:
+                    nc.scalar.copy(grouped_out[g, c][:, :, t], page[:, cols])
+
+        def quantize_out(g):
+            tag = "summed_then_scales" if g == 0 else "last_scales"
+            scales = keep.tile([P, T], U8, name="out_sc%d" % g, tag=tag, align_bytes=64)
+            words_hbm = out_1[g].rearrange("p t i -> p (t i)").bitcast(I32)
+            for c, cols in enumerate(chunks):
+                codes = ring.tile([P, CHUNK], I32, name="codes", align_bytes=64)
+                nc.vector.quantize_mx(
+                    out=codes[:].bitcast(FP8X4),
+                    scales=scales[:, cols],
+                    in_=grouped_out[g, c][:].rearrange("p j i -> p (j i)"),
+                )
+                nc.sync.dma_start(words_hbm[:, cols], codes[:])
+            for q in range(4):
+                nc.sync.dma_start(
+                    out_2[g, 4 * q : 4 * q + 4, :].bitcast(I32), scales[32 * q : 32 * q + 4, :].bitcast(I32)
+                )
+
+        for i in range(len(slices)):
+            if i + 2 < len(slices):
+                load_state(i + 2)
+                deal(i + 2)
+                product(i + 2, 0)
+                product(i + 2, 1)
+            place(i)
+            if i == 0:
+                late_page = keep.tile([P, T], F32, name="late_page", tag="state_then_page")
+                nc.gpsimd.memset(late_page[:], 0.0)
+                pages.append(late_page)
+            if i == PACK:
+                quantize_out(0)
+            hand_out(i)
+        quantize_out(1)

@@ -26,6 +26,8 @@ CHUNK = 512
 GROUPS = N // K_PASS
 BYTE_ORDER = (2, 0, 1, 3)
 PAGES = 3
+ROW0 = 96
+LOAD_AHEAD = 4
 VECTOR_CHUNKS = 2
 
 
@@ -47,44 +49,43 @@ def tile_list_tgn_rnnP_kernel(
         half_offsets = [offsets[:, h * (HALF // 16) : (h + 1) * (HALF // 16)] for h in range(J // HALF)]
 
         tab_sc = keep.tile([P, T], U8, name="tab_sc", align_bytes=64)
-        w_sc_raw = keep.tile([P, 2, N], U8, name="w_sc_raw", align_bytes=64)
-        v_sc1 = keep.tile([P, J], U8, name="v_sc1", align_bytes=64)
-        nc.vector.memset(tab_sc[:].bitcast(I32), 0)
-        nc.gpsimd.memset(w_sc_raw[:].bitcast(I32), 0)
-        nc.vector.memset(v_sc1[:].bitcast(I32), 0)
-        pages = [keep.tile([P, T], F32, name="page%d" % b) for b in range(PAGES - 1)]
-        for page in pages:
-            nc.vector.memset(page[:], 0.0)
+        w_sc_raw = keep.tile([P, N + K_PASS], U8, name="w_sc_raw", align_bytes=64)
+        staged = keep.tile([P, J + N + K_PASS], U8, name="staged", align_bytes=64)
+        planes = keep.tile([P, 2, J + N + K_PASS], U8, name="planes", align_bytes=64)
+        nc.sync.dma_start(tab_sc[ROW0:P, :].bitcast(I32), tab_scales.rearrange("a q t -> q a t").bitcast(I32))
+        nc.sync.dma_start(w_sc_raw[ROW0:P, 0:N].bitcast(I32), un_scales.rearrange("a q n -> q a n").bitcast(I32))
+        nc.sync.dma_start(
+            w_sc_raw[ROW0:P, N : N + K_PASS].bitcast(I32),
+            wn_scales[0].rearrange("q (g n) -> (q g) n", g=GROUPS).bitcast(I32),
+        )
+        nc.gpsimd.memset(tab_sc[0:ROW0, :].bitcast(I32), 0)
+        nc.gpsimd.memset(w_sc_raw[0:ROW0, :].bitcast(I32), 0)
+        pages = [keep.tile([P, T], F32, name="page0")]
+        nc.gpsimd.memset(planes[:].bitcast(I32), 0)
+        nc.vector.memset(pages[0][:].bitcast(I32), 0)
 
-        for q in range(4):
-            nc.sync.dma_start(
-                tab_sc[32 * q : 32 * q + 8, :].bitcast(I32), tab_scales[:, 4 * q : 4 * q + 4, :].bitcast(I32)
-            )
         tab_w = keep.tile([P, T], I32, name="tab_w", align_bytes=64)
         nc.sync.dma_start(tab_w[:], tab_words[0].rearrange("p t i -> p (t i)").bitcast(I32))
-        for q in range(4):
-            nc.sync.dma_start(
-                w_sc_raw[32 * q : 32 * q + 4, :, :].bitcast(I32),
-                un_scales[:, 4 * q : 4 * q + 4, :].rearrange("a r n -> r a n").bitcast(I32),
-            )
-            nc.sync.dma_start(
-                w_sc_raw[32 * q + 4 : 32 * q + 8, 0, :].bitcast(I32), wn_scales[0, 4 * q : 4 * q + 4, :].bitcast(I32)
-            )
 
         x_rows = x.rearrange("(p i) j -> p i j", i=PACK)
-        x_raw = [keep.tile([P, PACK, QUARTER], F32, name="x_raw%d" % c) for c in range(J // QUARTER)]
+        x_raw = {}
 
         def load_x(c):
+            x_raw[c] = keep.tile([P, PACK, QUARTER], F32, name="x_raw", tag="x_raw%d" % c, align_bytes=64)
             nc.sync.dma_start(x_raw[c][:], x_rows[:, :, c * QUARTER : (c + 1) * QUARTER])
 
         un_i32 = un_words.rearrange("a p n i -> p a (n i)").bitcast(I32)
         wn_i32 = wn_words[0].rearrange("p n i -> p (n i)").bitcast(I32)
-        w_raw = [keep.tile([P, 3, K_PASS], U32, name="w_raw%d" % g) for g in range(GROUPS)]
+        un_raw = {}
+        wn_raw = {}
 
-        def load_w(g):
-            cols = slice(g * K_PASS, (g + 1) * K_PASS)
-            nc.sync.dma_start(w_raw[g][:, 0:2, :].bitcast(I32), un_i32[:, :, cols])
-            nc.sync.dma_start(w_raw[g][:, 2, :].bitcast(I32), wn_i32[:, cols])
+        def load_un(g):
+            un_raw[g] = keep.tile([P, 2, K_PASS], U32, name="un_raw", tag="un_raw%d" % g)
+            nc.sync.dma_start(un_raw[g][:].bitcast(I32), un_i32[:, :, g * K_PASS : (g + 1) * K_PASS])
+
+        def load_wn(g):
+            wn_raw[g] = keep.tile([P, K_PASS], U32, name="wn_raw%d" % g)
+            nc.sync.dma_start(wn_raw[g][:].bitcast(I32), wn_i32[:, g * K_PASS : (g + 1) * K_PASS])
 
         h_rows = hT.rearrange("(g p t) c -> g t p c", p=P, t=PACK)
         out_rows = out_0.rearrange("(g p t) c -> g t p c", p=P, t=PACK)
@@ -92,122 +93,123 @@ def tile_list_tgn_rnnP_kernel(
 
         def load_state(i):
             g, t = slices[i]
-            if i == 0:
-                state[i] = keep.tile([P, T], F32, name="state_first", tag="state_then_page")
-            else:
-                state[i] = ring.tile([P, T], F32, name="state")
+            state[i] = ring.tile([P, T], F32, name="state", bufs=5)
             nc.sync.dma_start(state[i][:], h_rows[g, t])
 
-        weight = keep.tile([P, J], F32, name="weight")
         bias = keep.tile([P, GROUPS, PACK], F32, name="bias")
 
+        weight = keep.tile([P, J], F32, name="weight")
+        picked_sc = keep.tile([P, J], U8, name="picked_sc", align_bytes=64)
+
         load_x(0)
+        load_un(0)
         load_x(1)
-        load_w(0)
+        load_wn(0)
         nc.sync.dma_start(bias[:], bn.rearrange("(g p t) -> p g t", p=P, t=PACK))
+        nc.vector.tensor_copy(picked_sc[:], tab_sc[:].indirect(offsets[:]))
+        nc.vector.tensor_copy(
+            staged[:, J:].rearrange("p (b t m) -> p t b m", t=PACK, m=P),
+            w_sc_raw[:].rearrange("p (b m t) -> p t b m", t=PACK, m=P),
+        )
+        nc.vector.tensor_copy(staged[:, 0:J].bitcast(I32), picked_sc[:].bitcast(I32))
+        for q in range(4):
+            nc.sync.dma_start(
+                planes[32 * q : 32 * q + 4, :, :].bitcast(I32), staged[ROW0 + 8 * q : ROW0 + 8 * q + 8, :].bitcast(I32)
+            )
         load_state(0)
         nc.sync.dma_start(weight[:, halves[0]], wgo[:, halves[0]])
-
-        v_sc0 = keep.tile([P, J], U8, name="v_sc0", align_bytes=64)
-        nc.vector.tensor_copy(v_sc0[:], tab_sc[:].indirect(offsets[:]))
-        for q in range(4):
-            nc.sync.dma_start(v_sc1[32 * q : 32 * q + 4, :].bitcast(I32), v_sc0[32 * q + 4 : 32 * q + 8, :].bitcast(I32))
-        v_sc = [v_sc0, v_sc1]
-
         load_x(2)
         load_x(3)
-        nc.sync.dma_start(weight[:, halves[1]], wgo[:, halves[1]])
         load_state(1)
-        load_w(1)
+        load_un(1)
+        load_wn(1)
+        nc.sync.dma_start(weight[:, halves[1]], wgo[:, halves[1]])
+        load_state(2)
+        load_state(3)
 
-        w_sc = keep.tile([P, 2, N], U8, name="w_sc", align_bytes=64)
         v_words = [keep.tile([P, 2, HALF], U16, name="v_words%d" % h, align_bytes=64) for h in range(2)]
-        x_codes = [keep.tile([P, HALF], U32, name="x_codes%d" % h, align_bytes=64) for h in range(2)]
+        x_codes = {}
         x_sc = [keep.tile([P, HALF], U8, name="x_sc%d" % h, align_bytes=64) for h in range(2)]
 
         def gather_table(h):
-            picked = keep.tile([P, HALF], U32, name="picked%d" % h, align_bytes=64)
+            picked = keep.tile([P, HALF], U32, name="picked", tag="picked%d" % h, align_bytes=64)
             nc.vector.tensor_copy(picked[:], tab_w[:].bitcast(U32).indirect(half_offsets[h]))
             nc.vector.tensor_copy(v_words[h][:], picked[:].bitcast(U16).rearrange("p (j d) -> p d j", d=2))
 
         def quantize_x(h):
-            grouped = keep.tile([P, HALF, PACK], BF16, name="x_grouped%d" % h, align_bytes=64)
+            grouped = keep.tile([P, HALF, PACK], BF16, name="x_grouped", tag="x_grouped%d" % h, align_bytes=64)
             for c in range(2):
                 nc.scalar.copy(
                     grouped[:, c * QUARTER : (c + 1) * QUARTER, :].rearrange("p (c u) i -> p c i u", u=4),
                     x_raw[2 * h + c][:].rearrange("p i (c u) -> p c i u", u=4),
                 )
+            x_codes[h] = keep.tile([P, HALF], U32, name="x_codes", tag="x_codes%d" % h, align_bytes=64)
             nc.vector.quantize_mx(
                 out=x_codes[h][:].bitcast(FP8X4), scales=x_sc[h][:], in_=grouped[:].rearrange("p j i -> p (j i)")
             )
 
-        w_dealt = {}
+        un_dealt = {}
+        wn_dealt = {}
         act = {}
 
         def deal(i):
             g, t = slices[i]
-            w_dealt[i] = keep.tile([P, 3, P], U32, name="w_dealt%d" % i, align_bytes=64)
-            nc.scalar.copy(w_dealt[i][:], w_raw[g][:].rearrange("p a (m t) -> p a t m", t=PACK)[:, :, t, :])
-            act[i] = ring.tile([P, J], F32, name="act")
+            tag = "x_raw%d" % i if i in (2, 3) else "un_dealt%d" % i
+            un_dealt[i] = keep.tile([P, 2, P], U32, name="un_dealt", tag=tag, align_bytes=64)
+            wn_dealt[i] = keep.tile([P, P], U32, name="wn_dealt%d" % i, align_bytes=64)
+            nc.scalar.copy(un_dealt[i][:], un_raw[g][:].rearrange("p a (m t) -> p a t m", t=PACK)[:, :, t, :])
+            nc.scalar.copy(wn_dealt[i][:], wn_raw[g][:].rearrange("p (m t) -> p t m", t=PACK)[:, t, :])
 
         def product(i, h):
             g, t = slices[i]
-            cols = slice(g * K_PASS + t * P, g * K_PASS + (t + 1) * P)
+            un_col = J + g * K_PASS + t * P
+            wn_col = J + N + t * P
             acc = psum.tile([P, HALF], F32, name="acc")
             for a in range(2):
                 nc.tensor.matmul_mx(
                     out=acc[:],
-                    lhsT=w_dealt[i][:, a, :].bitcast(FP8X4),
-                    lhsT_scale=w_sc[:, a, cols],
+                    lhsT=un_dealt[i][:, a, :].bitcast(FP8X4),
+                    lhsT_scale=planes[:, a, un_col : un_col + P],
                     rhs=v_words[h][:, a, :].bitcast(FP4X4),
-                    rhs_scale=v_sc[a][:, halves[h]],
+                    rhs_scale=planes[:, a, halves[h]],
                     start=(a == 0),
                     stop=False,
                 )
             nc.tensor.matmul_mx(
                 out=acc[:],
-                lhsT=w_dealt[i][:, 2, :].bitcast(FP8X4),
-                lhsT_scale=w_sc[4:P, 0, cols],
+                lhsT=wn_dealt[i][:].bitcast(FP8X4),
+                lhsT_scale=planes[:, g, wn_col : wn_col + P],
                 rhs=x_codes[h][:].bitcast(FP8X4),
                 rhs_scale=x_sc[h][:],
                 start=False,
                 stop=True,
             )
-            nc.scalar.activation(act[i][:, halves[h]], acc[:], TANH, bias=bias[:, g, t : t + 1])
-
-        gather_table(0)
-        nc.vector.tensor_copy(
-            w_sc[:].rearrange("p a (g t m) -> p (a g) t m", t=PACK, m=P),
-            w_sc_raw[:].rearrange("p a (g m t) -> p (a g) t m", t=PACK, m=P),
-        )
-        quantize_x(0)
-        deal(0)
-        product(0, 0)
-        gather_table(1)
-        quantize_x(1)
-        product(0, 1)
-        deal(1)
-        product(1, 0)
-        product(1, 1)
+            if i == 0:
+                first = keep.tile([P, HALF], F32, name="act_first", tag=("x_grouped1", "act0")[h], align_bytes=64)
+                act[i, h] = first[:]
+            else:
+                if h == 0:
+                    act[i] = keep.tile([P, J], F32, name="act%d" % i)
+                act[i, h] = act[i][:, halves[h]]
+            nc.scalar.activation(act[i, h], acc[:], TANH, bias=bias[:, g, t : t + 1])
 
         grouped_out = {}
-        summed = {}
 
-        def place(i):
-            page = pages[i % PAGES]
-            if i == PACK:
-                summed[i] = keep.tile([P, J], F32, name="summed_mid", tag="summed_then_scales", align_bytes=64)
+        def pick(i, cols, offs_part, tanh_part, tag=None):
+            if tag:
+                summed = keep.tile([P, J], F32, name="summed_held", tag=tag, align_bytes=64)
             else:
-                summed[i] = ring.tile([P, J], F32, name="summed", bufs=2)
-            parts = list(zip(halves, half_offsets)) if i == 0 else [(slice(0, J), offsets[:])]
-            for cols, offs_part in parts:
-                nc.vector.tensor_tensor(summed[i][:, cols], state[i][:].indirect(offs_part), act[i][:, cols], ADD)
-                nc.vector.tensor_tensor(page[:].indirect(offs_part), summed[i][:, cols], weight[:, cols], MULT)
+                summed = ring.tile([P, J], F32, name="summed", bufs=2)
+            nc.vector.tensor_tensor(summed[:, cols], state[i][:].indirect(offs_part), tanh_part, ADD)
+            return summed
+
+        def put(i, cols, offs_part, summed):
+            nc.vector.tensor_tensor(pages[i % PAGES][:].indirect(offs_part), summed[:, cols], weight[:, cols], MULT)
 
         def hand_out(i):
             g, t = slices[i]
             page = pages[i % PAGES]
-            nc.scalar.dma_start(out_rows[g, t], page[:])
+            nc.sync.dma_start(out_rows[g, t], page[:])
             for c, cols in enumerate(chunks):
                 if (g, c) not in grouped_out:
                     grouped_out[g, c] = keep.tile([P, CHUNK, PACK], BF16, name="grouped%d_%d" % (g, c), align_bytes=64)
@@ -228,22 +230,50 @@ def tile_list_tgn_rnnP_kernel(
                     in_=grouped_out[g, c][:].rearrange("p j i -> p (j i)"),
                 )
                 nc.sync.dma_start(words_hbm[:, cols], codes[:])
+            queue = nc.scalar if g == GROUPS - 1 else nc.sync
             for q in range(4):
-                nc.sync.dma_start(
+                queue.dma_start(
                     out_2[g, 4 * q : 4 * q + 4, :].bitcast(I32), scales[32 * q : 32 * q + 4, :].bitcast(I32)
                 )
 
-        for i in range(len(slices)):
-            if i + 2 < len(slices):
-                load_state(i + 2)
-                deal(i + 2)
-                product(i + 2, 0)
-                product(i + 2, 1)
-            place(i)
-            if i == 0:
-                late_page = keep.tile([P, T], F32, name="late_page", tag="state_then_page")
-                nc.gpsimd.memset(late_page[:], 0.0)
-                pages.append(late_page)
+        gather_table(0)
+        deal(0)
+        quantize_x(0)
+        second_page = keep.tile([P, T], F32, name="page1", tag="x_grouped0", align_bytes=64)
+        nc.gpsimd.memset(second_page[:].bitcast(I32), 0)
+        pages.append(second_page)
+        product(0, 0)
+        gather_table(1)
+        deal(1)
+        product(1, 0)
+        put(0, halves[0], half_offsets[0], pick(0, halves[0], half_offsets[0], act[0, 0], "x_codes1"))
+        quantize_x(1)
+        product(0, 1)
+        product(1, 1)
+        put(1, halves[0], half_offsets[0], pick(1, halves[0], half_offsets[0], act[1, 0], "x_grouped1"))
+        put(0, halves[1], half_offsets[1], pick(0, halves[1], half_offsets[1], act[0, 1]))
+        for i in range(2, len(slices)):
+            deal(i)
+            if i == PACK - 1:
+                third_page = keep.tile([P, T], F32, name="page2", tag="un_raw0")
+                nc.gpsimd.memset(third_page[:].bitcast(I32), 0)
+                pages.append(third_page)
+            product(i, 0)
+            product(i, 1)
+        load_state(LOAD_AHEAD)
+        hand_out(0)
+        whole = slice(0, J)
+        waiting = pick(1, halves[1], half_offsets[1], act[1, 1])
+        for i in range(1, len(slices)):
+            tag = "summed_then_scales" if i + 1 == PACK else None
+            following = pick(i + 1, whole, offsets[:], act[i + 1][:], tag) if i + 1 < len(slices) else None
+            if i == 1:
+                put(i, halves[1], half_offsets[1], waiting)
+            else:
+                put(i, whole, offsets[:], waiting)
+            waiting = following
+            if i + LOAD_AHEAD < len(slices):
+                load_state(i + LOAD_AHEAD)
             if i == PACK:
                 quantize_out(0)
             hand_out(i)

from contextlib import ExitStack

import concourse.mybir as mybir

K, M, N, T, J = 512, 1024, 1024, 2048, 1024
FLOPS = 2 * (K + M) * N * J

F32 = mybir.dt.float32
BF16 = mybir.dt.bfloat16
I32 = mybir.dt.int32
U32 = mybir.dt.uint32
U16 = mybir.dt.uint16
U8 = mybir.dt.uint8
FP8X4 = mybir.dt.float8_e4m3fn_x4
FP4X4 = mybir.dt.float4_e2m1fn_x4
ADD = mybir.AluOpType.add
MULT = mybir.AluOpType.mult
TANH = mybir.ActivationFunctionType.Tanh

P = 128
PACK = 4
K_PASS = P * PACK
HALF = 512
QUARTER = 256
CHUNK = 512
GROUPS = N // K_PASS
BYTE_ORDER = (2, 0, 1, 3)
PAGES = 3
ROW0 = 96
LOAD_AHEAD = 4
VECTOR_CHUNKS = 2


def tile_list_tgn_rnnP_kernel(
    tc, x, tab_words, tab_scales, wn_words, wn_scales, un_words, un_scales, bn, hT, wgo, offs, out_0, out_1, out_2
):
    nc = tc.nc
    slices = [(g, t) for g in range(GROUPS) for t in BYTE_ORDER]
    halves = [slice(h * HALF, (h + 1) * HALF) for h in range(J // HALF)]
    chunks = [slice(c * CHUNK, (c + 1) * CHUNK) for c in range(T // CHUNK)]

    with ExitStack() as ctx:
        keep = ctx.enter_context(tc.tile_pool(name="keep", bufs=1))
        ring = ctx.enter_context(tc.tile_pool(name="ring", bufs=4))
        psum = ctx.enter_context(tc.psum_pool(name="psum", bufs=8))

        offsets = keep.tile([P, J // 16], U16, name="offsets")
        nc.sync.dma_start(offsets[:], offs)
        half_offsets = [offsets[:, h * (HALF // 16) : (h + 1) * (HALF // 16)] for h in range(J // HALF)]

        tab_sc = keep.tile([P, T], U8, name="tab_sc", align_bytes=64)
        w_sc_raw = keep.tile([P, N + K_PASS], U8, name="w_sc_raw", align_bytes=64)
        staged = keep.tile([P, J + N + K_PASS], U8, name="staged", align_bytes=64)
        planes = keep.tile([P, 2, J + N + K_PASS], U8, name="planes", align_bytes=64)
        nc.sync.dma_start(tab_sc[ROW0:P, :].bitcast(I32), tab_scales.rearrange("a q t -> q a t").bitcast(I32))
        nc.sync.dma_start(w_sc_raw[ROW0:P, 0:N].bitcast(I32), un_scales.rearrange("a q n -> q a n").bitcast(I32))
        nc.sync.dma_start(
            w_sc_raw[ROW0:P, N : N + K_PASS].bitcast(I32),
            wn_scales[0].rearrange("q (g n) -> (q g) n", g=GROUPS).bitcast(I32),
        )
        nc.gpsimd.memset(tab_sc[0:ROW0, :].bitcast(I32), 0)
        nc.gpsimd.memset(w_sc_raw[0:ROW0, :].bitcast(I32), 0)
        pages = [keep.tile([P, T], F32, name="page0")]
        nc.gpsimd.memset(planes[:].bitcast(I32), 0)
        nc.vector.memset(pages[0][:].bitcast(I32), 0)

        tab_w = keep.tile([P, T], I32, name="tab_w", align_bytes=64)
        nc.sync.dma_start(tab_w[:], tab_words[0].rearrange("p t i -> p (t i)").bitcast(I32))

        x_rows = x.rearrange("(p i) j -> p i j", i=PACK)
        x_raw = {}

        def load_x(c):
            x_raw[c] = keep.tile([P, PACK, QUARTER], F32, name="x_raw", tag="x_raw%d" % c, align_bytes=64)
            nc.sync.dma_start(x_raw[c][:], x_rows[:, :, c * QUARTER : (c + 1) * QUARTER])

        un_i32 = un_words.rearrange("a p n i -> p a (n i)").bitcast(I32)
        wn_i32 = wn_words[0].rearrange("p n i -> p (n i)").bitcast(I32)
        un_raw = {}
        wn_raw = {}

        def load_un(g):
            un_raw[g] = keep.tile([P, 2, K_PASS], U32, name="un_raw", tag="un_raw%d" % g)
            nc.sync.dma_start(un_raw[g][:].bitcast(I32), un_i32[:, :, g * K_PASS : (g + 1) * K_PASS])

        def load_wn(g):
            wn_raw[g] = keep.tile([P, K_PASS], U32, name="wn_raw%d" % g)
            nc.sync.dma_start(wn_raw[g][:].bitcast(I32), wn_i32[:, g * K_PASS : (g + 1) * K_PASS])

        h_rows = hT.rearrange("(g p t) c -> g t p c", p=P, t=PACK)
        out_rows = out_0.rearrange("(g p t) c -> g t p c", p=P, t=PACK)
        state = {}

        def load_state(i):
            g, t = slices[i]
            state[i] = ring.tile([P, T], F32, name="state", bufs=5)
            nc.sync.dma_start(state[i][:], h_rows[g, t])

        bias = keep.tile([P, GROUPS, PACK], F32, name="bias")

        weight = keep.tile([P, J], F32, name="weight")
        picked_sc = keep.tile([P, J], U8, name="picked_sc", align_bytes=64)

        load_x(0)
        load_un(0)
        load_x(1)
        load_wn(0)
        nc.sync.dma_start(bias[:], bn.rearrange("(g p t) -> p g t", p=P, t=PACK))
        nc.vector.tensor_copy(picked_sc[:], tab_sc[:].indirect(offsets[:]))
        nc.vector.tensor_copy(
            staged[:, J:].rearrange("p (b t m) -> p t b m", t=PACK, m=P),
            w_sc_raw[:].rearrange("p (b m t) -> p t b m", t=PACK, m=P),
        )
        nc.vector.tensor_copy(staged[:, 0:J].bitcast(I32), picked_sc[:].bitcast(I32))
        for q in range(4):
            nc.sync.dma_start(
                planes[32 * q : 32 * q + 4, :, :].bitcast(I32), staged[ROW0 + 8 * q : ROW0 + 8 * q + 8, :].bitcast(I32)
            )
        load_state(0)
        nc.sync.dma_start(weight[:, halves[0]], wgo[:, halves[0]])
        load_x(2)
        load_x(3)
        load_state(1)
        load_un(1)
        load_wn(1)
        nc.sync.dma_start(weight[:, halves[1]], wgo[:, halves[1]])
        load_state(2)
        load_state(3)

        v_words = [keep.tile([P, 2, HALF], U16, name="v_words%d" % h, align_bytes=64) for h in range(2)]
        x_codes = {}
        x_sc = [keep.tile([P, HALF], U8, name="x_sc%d" % h, align_bytes=64) for h in range(2)]

        def gather_table(h):
            picked = keep.tile([P, HALF], U32, name="picked", tag="picked%d" % h, align_bytes=64)
            nc.vector.tensor_copy(picked[:], tab_w[:].bitcast(U32).indirect(half_offsets[h]))
            nc.vector.tensor_copy(v_words[h][:], picked[:].bitcast(U16).rearrange("p (j d) -> p d j", d=2))

        def quantize_x(h):
            grouped = keep.tile([P, HALF, PACK], BF16, name="x_grouped", tag="x_grouped%d" % h, align_bytes=64)
            for c in range(2):
                nc.scalar.copy(
                    grouped[:, c * QUARTER : (c + 1) * QUARTER, :].rearrange("p (c u) i -> p c i u", u=4),
                    x_raw[2 * h + c][:].rearrange("p i (c u) -> p c i u", u=4),
                )
            x_codes[h] = keep.tile([P, HALF], U32, name="x_codes", tag="x_codes%d" % h, align_bytes=64)
            nc.vector.quantize_mx(
                out=x_codes[h][:].bitcast(FP8X4), scales=x_sc[h][:], in_=grouped[:].rearrange("p j i -> p (j i)")
            )

        un_dealt = {}
        wn_dealt = {}
        act = {}

        def deal(i):
            g, t = slices[i]
            tag = "x_raw%d" % i if i in (2, 3) else "un_dealt%d" % i
            un_dealt[i] = keep.tile([P, 2, P], U32, name="un_dealt", tag=tag, align_bytes=64)
            wn_dealt[i] = keep.tile([P, P], U32, name="wn_dealt%d" % i, align_bytes=64)
            nc.scalar.copy(un_dealt[i][:], un_raw[g][:].rearrange("p a (m t) -> p a t m", t=PACK)[:, :, t, :])
            nc.scalar.copy(wn_dealt[i][:], wn_raw[g][:].rearrange("p (m t) -> p t m", t=PACK)[:, t, :])

        def product(i, h):
            g, t = slices[i]
            un_col = J + g * K_PASS + t * P
            wn_col = J + N + t * P
            acc = psum.tile([P, HALF], F32, name="acc")
            for a in range(2):
                nc.tensor.matmul_mx(
                    out=acc[:],
                    lhsT=un_dealt[i][:, a, :].bitcast(FP8X4),
                    lhsT_scale=planes[:, a, un_col : un_col + P],
                    rhs=v_words[h][:, a, :].bitcast(FP4X4),
                    rhs_scale=planes[:, a, halves[h]],
                    start=(a == 0),
                    stop=False,
                )
            nc.tensor.matmul_mx(
                out=acc[:],
                lhsT=wn_dealt[i][:].bitcast(FP8X4),
                lhsT_scale=planes[:, g, wn_col : wn_col + P],
                rhs=x_codes[h][:].bitcast(FP8X4),
                rhs_scale=x_sc[h][:],
                start=False,
                stop=True,
            )
            if i == 0:
                first = keep.tile([P, HALF], F32, name="act_first", tag=("x_grouped1", "act0")[h], align_bytes=64)
                act[i, h] = first[:]
            else:
                if h == 0:
                    act[i] = keep.tile([P, J], F32, name="act%d" % i)
                act[i, h] = act[i][:, halves[h]]
            nc.scalar.activation(act[i, h], acc[:], TANH, bias=bias[:, g, t : t + 1])

        grouped_out = {}

        def pick(i, cols, offs_part, tanh_part, tag=None):
            if tag:
                summed = keep.tile([P, J], F32, name="summed_held", tag=tag, align_bytes=64)
            else:
                summed = ring.tile([P, J], F32, name="summed", bufs=2)
            nc.vector.tensor_tensor(summed[:, cols], state[i][:].indirect(offs_part), tanh_part, ADD)
            return summed

        def put(i, cols, offs_part, summed):
            nc.vector.tensor_tensor(pages[i % PAGES][:].indirect(offs_part), summed[:, cols], weight[:, cols], MULT)

        def hand_out(i):
            g, t = slices[i]
            page = pages[i % PAGES]
            nc.sync.dma_start(out_rows[g, t], page[:])
            for c, cols in enumerate(chunks):
                if (g, c) not in grouped_out:
                    grouped_out[g, c] = keep.tile([P, CHUNK, PACK], BF16, name="grouped%d_%d" % (g, c), align_bytes=64)
                if i == len(slices) - 1 and c < VECTOR_CHUNKS:
                    nc.vector.tensor_copy(grouped_out[g, c][:, :, t], page[:, cols])
                else:
                    nc.scalar.copy(grouped_out[g, c][:, :, t], page[:, cols])

        def quantize_out(g):
            tag = "summed_then_scales" if g == 0 else "last_scales"
            scales = keep.tile([P, T], U8, name="out_sc%d" % g, tag=tag, align_bytes=64)
            words_hbm = out_1[g].rearrange("p t i -> p (t i)").bitcast(I32)
            for c, cols in enumerate(chunks):
                codes = ring.tile([P, CHUNK], I32, name="codes", align_bytes=64)
                nc.vector.quantize_mx(
                    out=codes[:].bitcast(FP8X4),
                    scales=scales[:, cols],
                    in_=grouped_out[g, c][:].rearrange("p j i -> p (j i)"),
                )
                nc.sync.dma_start(words_hbm[:, cols], codes[:])
            queue = nc.scalar if g == GROUPS - 1 else nc.sync
            for q in range(4):
                queue.dma_start(
                    out_2[g, 4 * q : 4 * q + 4, :].bitcast(I32), scales[32 * q : 32 * q + 4, :].bitcast(I32)
                )

        gather_table(0)
        deal(0)
        quantize_x(0)
        second_page = keep.tile([P, T], F32, name="page1", tag="x_grouped0", align_bytes=64)
        nc.gpsimd.memset(second_page[:].bitcast(I32), 0)
        pages.append(second_page)
        product(0, 0)
        gather_table(1)
        deal(1)
        product(1, 0)
        put(0, halves[0], half_offsets[0], pick(0, halves[0], half_offsets[0], act[0, 0], "x_codes1"))
        quantize_x(1)
        product(0, 1)
        product(1, 1)
        put(1, halves[0], half_offsets[0], pick(1, halves[0], half_offsets[0], act[1, 0], "x_grouped1"))
        put(0, halves[1], half_offsets[1], pick(0, halves[1], half_offsets[1], act[0, 1]))
        for i in range(2, len(slices)):
            deal(i)
            if i == PACK - 1:
                third_page = keep.tile([P, T], F32, name="page2", tag="un_raw0")
                nc.gpsimd.memset(third_page[:].bitcast(I32), 0)
                pages.append(third_page)
            product(i, 0)
            product(i, 1)
        load_state(LOAD_AHEAD)
        hand_out(0)
        whole = slice(0, J)
        waiting = pick(1, halves[1], half_offsets[1], act[1, 1])
        for i in range(1, len(slices)):
            tag = "summed_then_scales" if i + 1 == PACK else None
            following = pick(i + 1, whole, offsets[:], act[i + 1][:], tag) if i + 1 < len(slices) else None
            if i == 1:
                put(i, halves[1], half_offsets[1], waiting)
            else:
                put(i, whole, offsets[:], waiting)
            waiting = following
            if i + LOAD_AHEAD < len(slices):
                load_state(i + LOAD_AHEAD)
            if i == PACK:
                quantize_out(0)
            hand_out(i)
        quantize_out(1)
